import numpy as np
import ml_dtypes


def mxq(x, axis, fmt="e4m3"):
    dtype, down = {"e4m3": (ml_dtypes.float8_e4m3fn, 7), "e5m2": (ml_dtypes.float8_e5m2, 14)}[fmt]
    v = np.moveaxis(np.asarray(x, np.float32).astype(ml_dtypes.bfloat16).astype(np.float64), axis, -1)
    blocks = v.reshape(v.shape[:-1] + (-1, 32))
    amax = np.abs(blocks).max(-1, keepdims=True)
    byte = np.maximum(np.where(amax > 0, np.frexp(amax)[1] - 1 + 127, 0) - down, 1)
    scale = np.exp2(byte - 127.0)
    codes = (blocks / scale).astype(np.float32).astype(dtype).astype(np.float64)
    return np.moveaxis((codes * scale).reshape(v.shape), -1, axis)


WIDE = False


def mx_kscale(k):
    if not WIDE:
        return np.ones(k)
    levels = np.array([10, -10, 5, -5, 0])
    if k % 512:
        return np.exp2(np.random.permutation(np.resize(levels, k // 32))).repeat(32)
    a = np.empty((k // 512, 16))
    for p in range(k // 512):
        a[p, :8] = np.random.permutation(np.resize(levels, 8))
        for g in range(8):
            far = levels[np.abs(levels - a[p, g]) >= 10]
            a[p, g + 8] = far[np.random.randint(len(far))]
    return np.exp2(a.ravel()).repeat(32)


def f64(x):
    return np.asarray(x).astype(np.float64)


def striped(idx):
    return np.tile(idx.reshape(-1, 16).T, (8, 1)).astype(np.uint16)


def unstriped(offs):
    return offs[:16].T.reshape(-1).astype(np.int64)


def striped8(idx):
    return np.concatenate([x.reshape(-1, 16).T for x in idx]).astype(np.uint16)


def runs(offs, k):
    lists = np.stack([offs[16 * r : 16 * r + 16].T.reshape(-1) for r in range(8)]).astype(np.int64)
    return lists[np.arange(k) % 512 // 64]


def pack_weight(w):
    k, n = w.shape
    w = f64(np.asarray(w, np.float32).astype(ml_dtypes.bfloat16)).reshape(k // 32, 32, n)
    amax = np.abs(w).max(1)
    byte = np.clip(np.where(amax > 0, np.frexp(amax)[1] - 1 + 127 - 7, 1), 1, 254)
    scaled = (w * np.exp2(127.0 - byte)[:, None, :]).reshape(k, n).astype(np.float32)
    words = np.ascontiguousarray(scaled.reshape(k // 512, 128, 4, n).transpose(0, 1, 3, 2)).astype(ml_dtypes.float8_e4m3fn).view(np.uint8)
    return words, np.ascontiguousarray(byte.astype(np.uint8).reshape(k // 512, 16, n))


def unpack_weight(words, scales):
    g, p, n, _ = words.shape
    vals = np.ascontiguousarray(words).view(ml_dtypes.float8_e4m3fn).astype(np.float64) * np.repeat(np.exp2(scales.astype(np.float64) - 127.0), 8, axis=1)[..., None]
    return vals.transpose(0, 1, 3, 2).reshape(g * 512, n)


K, T, S, N, W = 512, 2048, 256, 512, 128


def setup_inputs():
    n = np.random.standard_normal
    s = mx_kscale(K)[:, None]
    packed_xT = pack_weight(n((K, T)) * s)
    perm = np.random.permutation(S)
    return {
        "x_words": packed_xT[0],
        "x_scales": packed_xT[1],
        "w1": (n((K, N)) / np.sqrt(2 * K) / s).astype(np.float32),
        "w2": (n((K, N)) / np.sqrt(2 * K) / s).astype(np.float32),
        "offs": striped8(np.random.randint(0, T, (8, S))),
        "hz": striped8(np.random.randint(0, T, (8, S))),
        "n1": striped(perm[:W]),
        "n2": striped(perm[W:]),
    }


def reference(x_words, x_scales, w1, w2, offs, hz, n1, n2):
    xq = unpack_weight(x_words, x_scales)[np.arange(K)[:, None], runs(offs, K)]
    x_hz = unpack_weight(x_words, x_scales)[np.arange(K)[:, None], runs(hz, K)]
    h = mxq(f64(w1), 0, "e4m3").T @ xq + mxq(f64(w2), 0, "e4m3").T @ x_hz
    pa = h[:, unstriped(n1)]
    pb = h[:, unstriped(n2)]
    rb = pa - pb
    ra = 0.75 * (pa + pb)
    ds = np.zeros((N, S))
    ds[:, unstriped(n1)] = ra
    out = ds.copy()
    out[:, unstriped(n2)] = rb
    return out

@@ -1,0 +1,149 @@
+from contextlib import ExitStack
+
+import concourse.mybir as mybir
+
+K, T, S, N, W = 512, 2048, 256, 512, 128
+FLOPS = 2 * 2 * K * N * S
+
+F32 = mybir.dt.float32
+BF16 = mybir.dt.bfloat16
+I32 = mybir.dt.int32
+U32 = mybir.dt.uint32
+U16 = mybir.dt.uint16
+U8 = mybir.dt.uint8
+FP8X4 = mybir.dt.float8_e4m3fn_x4
+COPY = mybir.ActivationFunctionType.Copy
+ADD = mybir.AluOpType.add
+SUB = mybir.AluOpType.subtract
+
+P = 128
+PACK = 4
+PIECES = ((0, 128), (128, 128), (256, 256))
+
+
+def tile_picked_ohhhaar_none_p_kernel(tc, x_words, x_scales, w1, w2, offs, hz, n1, n2, out):
+    nc = tc.nc
+    with ExitStack() as ctx:
+        keep = ctx.enter_context(tc.tile_pool(name="keep", bufs=1))
+        psum = ctx.enter_context(tc.psum_pool(name="psum", bufs=1))
+
+        def load_list(name, src):
+            tile = keep.tile(list(src.shape), U16, name=name)
+            nc.sync.dma_start(tile[:], src)
+            return tile
+
+        def load_weight(name, w, piece, tag=None, queue=nc.sync):
+            c0, width = PIECES[piece]
+            raw = keep.tile([P, PACK, width], F32, name=f"{name}_raw{piece}", tag=tag or f"{name}_raw{piece}", align_bytes=64)
+            queue.dma_start(out=raw[:], in_=w[:, c0 : c0 + width].rearrange("(p j) c -> p j c", j=PACK))
+            return raw
+
+        def interleave(name, raw, b, on_scalar, tag=None):
+            c0 = b * P - PIECES[min(b, 2)][0]
+            grouped = keep.tile([P, P, PACK], BF16, name=f"{name}_bf{b}", tag=tag or f"{name}_bf{b}", align_bytes=64)
+            dst = grouped[:].rearrange("p (c i) j -> p c j i", i=4)
+            src = raw[:, :, c0 : c0 + P].rearrange("p j (c i) -> p c j i", i=4)
+            if on_scalar:
+                nc.scalar.copy(out=dst, in_=src)
+            else:
+                nc.vector.tensor_copy(out=dst, in_=src)
+            return grouped
+
+        def quantise(name, grouped, b):
+            codes = keep.tile([P, P], U32, name=f"{name}_codes{b}", tag=f"{name}_codes{b}", align_bytes=64)
+            scales = keep.tile([P, P], U8, name=f"{name}_scales{b}", tag=f"{name}_scales{b}", align_bytes=64)
+            nc.vector.quantize_mx(out=codes[:].bitcast(FP8X4), scales=scales[:], in_=grouped[:].rearrange("p c j -> p (c j)"))
+            return codes, scales
+
+        scale_table = keep.tile([P, T], U8, name="scale_table", tag="scale_table", align_bytes=64)
+        nc.vector.memset(scale_table[:].bitcast(I32), 0)
+        x_plane = keep.tile([P, 2 * S], U8, name="x_plane", align_bytes=64)
+        nc.vector.memset(x_plane[:].bitcast(I32), 0)
+        offs_t = load_list("offs_t", offs)
+        w1_raw = [load_weight("w1", w1, 0, queue=nc.scalar)]
+        hz_t = load_list("hz_t", hz)
+        n1_t = load_list("n1_t", n1)
+        n2_t = load_list("n2_t", n2)
+        scale_rows = x_scales[0].bitcast(I32).rearrange("(r e) c -> e r c", e=2)
+        for e in range(2):
+            nc.sync.dma_start(out=scale_table[e:P:16, :].bitcast(I32), in_=scale_rows[e])
+
+        word_table = keep.tile([P, T], U32, name="word_table", align_bytes=64)
+        nc.sync.dma_start(out=word_table[:].bitcast(I32), in_=x_words[0].rearrange("p c r -> p (c r)").bitcast(I32))
+        w2_raw = [load_weight("w2", w2, 0)]
+        w1_raw.append(load_weight("w1", w1, 1))
+        w2_raw.append(load_weight("w2", w2, 1))
+
+        picked_bytes = keep.tile([P, 2 * S], U8, name="picked_bytes", tag="picked_bytes", align_bytes=64)
+        nc.vector.tensor_copy(picked_bytes[:, 0:S], scale_table[:].indirect(offs_t[:]))
+        nc.vector.tensor_copy(picked_bytes[:, S : 2 * S], scale_table[:].indirect(hz_t[:]))
+        w1_bf0 = interleave("w1", w1_raw[0], 0, True)
+        for e in range(2):
+            nc.scalar.dma_start(out=x_plane[2 + e : P : 32, :].bitcast(I32), in_=picked_bytes[16 + e : P : 32, :].bitcast(I32))
+        for q in range(0, P, 32):
+            nc.vector.tensor_copy(x_plane[q : q + 2, :].bitcast(I32), picked_bytes[q : q + 2, :].bitcast(I32))
+        w1_raw.append(load_weight("w1", w1, 2, "scale_table"))
+        w2_raw.append(load_weight("w2", w2, 2, "picked_bytes"))
+
+        w1_q = [quantise("w1", w1_bf0, 0)]
+        words_offs = keep.tile([P, S], U32, name="words_offs", align_bytes=64)
+        words_hz = keep.tile([P, S], U32, name="words_hz", align_bytes=64)
+        nc.vector.tensor_copy(words_offs[:], word_table[:].indirect(offs_t[:]))
+        w2_bf0 = interleave("w2", w2_raw[0], 0, True)
+        nc.vector.tensor_copy(words_hz[:], word_table[:].indirect(hz_t[:]))
+        w2_q = [quantise("w2", w2_bf0, 0)]
+
+        def product(b):
+            acc = psum.tile([P, S], F32, name=f"acc{b}")
+            nc.tensor.matmul_mx(
+                out=acc[:], lhsT=w1_q[b][0][:].bitcast(FP8X4), lhsT_scale=w1_q[b][1][:],
+                rhs=words_offs[:].bitcast(FP8X4), rhs_scale=x_plane[:, 0:S], start=True, stop=False)
+            nc.tensor.matmul_mx(
+                out=acc[:], lhsT=w2_q[b][0][:].bitcast(FP8X4), lhsT_scale=w2_q[b][1][:],
+                rhs=words_hz[:].bitcast(FP8X4), rhs_scale=x_plane[:, S : 2 * S], start=False, stop=True)
+            h = keep.tile([P, S], F32, name=f"h{b}", tag=f"h{b}", align_bytes=64)
+            nc.vector.tensor_copy(h[:], acc[:])
+            return h
+
+        def fetch(b, h):
+            pa = keep.tile([P, W], F32, name=f"pa{b}", align_bytes=64)
+            pb = keep.tile([P, W], F32, name=f"pb{b}", align_bytes=64)
+            nc.scalar.activation(pa[:], h[:].indirect(n1_t[:]), COPY)
+            nc.scalar.activation(pb[:], h[:].indirect(n2_t[:]), COPY)
+            return pa, pb
+
+        def put_sum(b, pa, pb):
+            total = keep.tile([P, W], F32, name=f"total{b}", align_bytes=64)
+            nc.vector.tensor_tensor(total[:], pa[:], pb[:], ADD)
+            result = keep.tile([P, S], F32, name=f"result{b}", align_bytes=64)
+            nc.scalar.activation(result[:].indirect(n1_t[:]), total[:], COPY, scale=0.75)
+            return result
+
+        def difference(b, pa, pb):
+            diff = keep.tile([P, W], F32, name=f"diff{b}", tag=f"w2_codes{min(b + 1, 3)}" if b < 3 else "diff3", align_bytes=64)
+            nc.vector.tensor_tensor(diff[:], pa[:], pb[:], SUB)
+            return diff
+
+        def put_difference(b, result, diff):
+            nc.scalar.activation(result[:].indirect(n2_t[:]), diff[:], COPY)
+            nc.sync.dma_start(out=out[b * P : (b + 1) * P, :], in_=result[:])
+
+        w1_tags = (None, None, "w2_scales1", "w2_scales1")
+        w2_tags = (None, "w2_codes0", "h1", "h1")
+
+        def prepare(b):
+            w1_bf = interleave("w1", w1_raw[min(b, 2)], b, False, w1_tags[b])
+            w2_bf = interleave("w2", w2_raw[min(b, 2)], b, False, w2_tags[b])
+            w1_q.append(quantise("w1", w1_bf, b))
+            w2_q.append(quantise("w2", w2_bf, b))
+
+        pair = fetch(0, product(0))
+        for b in range(4):
+            result = put_sum(b, *pair)
+            if b < 3:
+                prepare(b + 1)
+                h_next = product(b + 1)
+            diff = difference(b, *pair)
+            if b < 3:
+                pair = fetch(b + 1, h_next)
+            put_difference(b, result, diff)

@@ -18,7 +18,7 @@ SUB = mybir.AluOpType.subtract
 
 P = 128
 PACK = 4
-PIECES = ((0, 128), (128, 128), (256, 256))
+PIECES = ((0, 256), (256, 256))
 
 
 def tile_picked_ohhhaar_none_p_kernel(tc, x_words, x_scales, w1, w2, offs, hz, n1, n2, out):
@@ -39,7 +39,7 @@ def tile_picked_ohhhaar_none_p_kernel(tc, x_words, x_scales, w1, w2, offs, hz, n
             return raw
 
         def interleave(name, raw, b, on_scalar, tag=None):
-            c0 = b * P - PIECES[min(b, 2)][0]
+            c0 = b % 2 * P
             grouped = keep.tile([P, P, PACK], BF16, name=f"{name}_bf{b}", tag=tag or f"{name}_bf{b}", align_bytes=64)
             dst = grouped[:].rearrange("p (c i) j -> p c j i", i=4)
             src = raw[:, :, c0 : c0 + P].rearrange("p j (c i) -> p c j i", i=4)
@@ -71,8 +71,6 @@ def tile_picked_ohhhaar_none_p_kernel(tc, x_words, x_scales, w1, w2, offs, hz, n
         word_table = keep.tile([P, T], U32, name="word_table", align_bytes=64)
         nc.sync.dma_start(out=word_table[:].bitcast(I32), in_=x_words[0].rearrange("p c r -> p (c r)").bitcast(I32))
         w2_raw = [load_weight("w2", w2, 0)]
-        w1_raw.append(load_weight("w1", w1, 1))
-        w2_raw.append(load_weight("w2", w2, 1))
 
         picked_bytes = keep.tile([P, 2 * S], U8, name="picked_bytes", tag="picked_bytes", align_bytes=64)
         nc.vector.tensor_copy(picked_bytes[:, 0:S], scale_table[:].indirect(offs_t[:]))
@@ -82,16 +80,24 @@ def tile_picked_ohhhaar_none_p_kernel(tc, x_words, x_scales, w1, w2, offs, hz, n
             nc.scalar.dma_start(out=x_plane[2 + e : P : 32, :].bitcast(I32), in_=picked_bytes[16 + e : P : 32, :].bitcast(I32))
         for q in range(0, P, 32):
             nc.vector.tensor_copy(x_plane[q : q + 2, :].bitcast(I32), picked_bytes[q : q + 2, :].bitcast(I32))
-        w1_raw.append(load_weight("w1", w1, 2, "scale_table"))
-        w2_raw.append(load_weight("w2", w2, 2, "picked_bytes"))
+        late = keep.tile([P, 2 * PACK * (N - 2 * P)], F32, name="late", tag="scale_table", align_bytes=64)
+        at = 0
+        for c0, width in PIECES[1:]:
+            for w, raws in ((w1, w1_raw), (w2, w2_raw)):
+                raw = late[:, at : at + PACK * width].rearrange("p (j c) -> p j c", j=PACK)
+                nc.scalar.dma_start(out=raw, in_=w[:, c0 : c0 + width].rearrange("(p j) c -> p j c", j=PACK))
+                raws.append(raw)
+                at += PACK * width
 
-        w1_q = [quantise("w1", w1_bf0, 0)]
+        w1_bf1 = interleave("w1", w1_raw[0], 1, False)
+        w1_q = [quantise("w1", w1_bf0, 0), quantise("w1", w1_bf1, 1)]
         words_offs = keep.tile([P, S], U32, name="words_offs", align_bytes=64)
         words_hz = keep.tile([P, S], U32, name="words_hz", align_bytes=64)
         nc.vector.tensor_copy(words_offs[:], word_table[:].indirect(offs_t[:]))
-        w2_bf0 = interleave("w2", w2_raw[0], 0, True)
         nc.vector.tensor_copy(words_hz[:], word_table[:].indirect(hz_t[:]))
-        w2_q = [quantise("w2", w2_bf0, 0)]
+        w2_bf0 = interleave("w2", w2_raw[0], 0, False)
+        w2_bf1 = interleave("w2", w2_raw[0], 1, True)
+        w2_q = [quantise("w2", w2_bf0, 0), quantise("w2", w2_bf1, 1)]
 
         def product(b):
             acc = psum.tile([P, S], F32, name=f"acc{b}")
@@ -102,7 +108,10 @@ def tile_picked_ohhhaar_none_p_kernel(tc, x_words, x_scales, w1, w2, offs, hz, n
                 out=acc[:], lhsT=w2_q[b][0][:].bitcast(FP8X4), lhsT_scale=w2_q[b][1][:],
                 rhs=words_hz[:].bitcast(FP8X4), rhs_scale=x_plane[:, S : 2 * S], start=False, stop=True)
             h = keep.tile([P, S], F32, name=f"h{b}", tag=f"h{b}", align_bytes=64)
-            nc.vector.tensor_copy(h[:], acc[:])
+            if b == 0:
+                nc.scalar.copy(out=h[:], in_=acc[:])
+            else:
+                nc.vector.tensor_copy(h[:], acc[:])
             return h
 
         def fetch(b, h):
@@ -112,38 +121,39 @@ def tile_picked_ohhhaar_none_p_kernel(tc, x_words, x_scales, w1, w2, offs, hz, n
             nc.scalar.activation(pb[:], h[:].indirect(n2_t[:]), COPY)
             return pa, pb
 
-        def put_sum(b, pa, pb):
-            total = keep.tile([P, W], F32, name=f"total{b}", align_bytes=64)
-            nc.vector.tensor_tensor(total[:], pa[:], pb[:], ADD)
-            result = keep.tile([P, S], F32, name=f"result{b}", align_bytes=64)
-            nc.scalar.activation(result[:].indirect(n1_t[:]), total[:], COPY, scale=0.75)
-            return result
-
-        def difference(b, pa, pb):
-            diff = keep.tile([P, W], F32, name=f"diff{b}", tag=f"w2_codes{min(b + 1, 3)}" if b < 3 else "diff3", align_bytes=64)
-            nc.vector.tensor_tensor(diff[:], pa[:], pb[:], SUB)
-            return diff
-
-        def put_difference(b, result, diff):
-            nc.scalar.activation(result[:].indirect(n2_t[:]), diff[:], COPY)
-            nc.sync.dma_start(out=out[b * P : (b + 1) * P, :], in_=result[:])
-
-        w1_tags = (None, None, "w2_scales1", "w2_scales1")
-        w2_tags = (None, "w2_codes0", "h1", "h1")
+        def combine(name, b, pair, op, tag):
+            values = keep.tile([P, W], F32, name=f"{name}{b}", tag=tag, align_bytes=64)
+            nc.vector.tensor_tensor(values[:], pair[0][:], pair[1][:], op)
+            return values
 
         def prepare(b):
-            w1_bf = interleave("w1", w1_raw[min(b, 2)], b, False, w1_tags[b])
-            w2_bf = interleave("w2", w2_raw[min(b, 2)], b, False, w2_tags[b])
+            w1_bf = interleave("w1", w1_raw[1], b, False)
+            w2_bf = interleave("w2", w2_raw[1], b, False)
             w1_q.append(quantise("w1", w1_bf, b))
             w2_q.append(quantise("w2", w2_bf, b))
 
-        pair = fetch(0, product(0))
-        for b in range(4):
-            result = put_sum(b, *pair)
-            if b < 3:
-                prepare(b + 1)
-                h_next = product(b + 1)
-            diff = difference(b, *pair)
-            if b < 3:
-                pair = fetch(b + 1, h_next)
-            put_difference(b, result, diff)
+        def finish(a, h_a, h_b):
+            b = a + 1
+            pair_a = fetch(a, h_a)
+            pair_b = fetch(b, h_b)
+            total_a = combine("total", a, pair_a, ADD, f"w2_codes{b}")
+            total_b = combine("total", b, pair_b, ADD, f"total{b}")
+            diff_a = combine("diff", a, pair_a, SUB, f"h{b}")
+            diff_b = combine("diff", b, pair_b, SUB, f"diff{b}")
+            result_a = keep.tile([P, S], F32, name=f"result{a}", align_bytes=64)
+            result_b = keep.tile([P, S], F32, name=f"result{b}", align_bytes=64)
+            nc.scalar.activation(result_a[:].indirect(n1_t[:]), total_a[:], COPY, scale=0.75)
+            nc.scalar.activation(result_b[:].indirect(n1_t[:]), total_b[:], COPY, scale=0.75)
+            nc.scalar.activation(result_a[:].indirect(n2_t[:]), diff_a[:], COPY)
+            nc.sync.dma_start(out=out[a * P : (a + 1) * P, :], in_=result_a[:])
+            nc.scalar.activation(result_b[:].indirect(n2_t[:]), diff_b[:], COPY)
+            nc.sync.dma_start(out=out[b * P : (b + 1) * P, :], in_=result_b[:])
+
+        h0 = product(0)
+        h1 = product(1)
+        finish(0, h0, h1)
+        prepare(2)
+        h2 = product(2)
+        prepare(3)
+        h3 = product(3)
+        finish(2, h2, h3)

from contextlib import ExitStack

import concourse.mybir as mybir

K, T, S, N, W = 512, 2048, 256, 512, 128
FLOPS = 2 * 2 * K * N * S

F32 = mybir.dt.float32
BF16 = mybir.dt.bfloat16
I32 = mybir.dt.int32
U32 = mybir.dt.uint32
U16 = mybir.dt.uint16
U8 = mybir.dt.uint8
FP8X4 = mybir.dt.float8_e4m3fn_x4
COPY = mybir.ActivationFunctionType.Copy
ADD = mybir.AluOpType.add
SUB = mybir.AluOpType.subtract

P = 128
PACK = 4
PIECES = ((0, 256), (256, 256))


def tile_picked_ohhhaar_none_p_kernel(tc, x_words, x_scales, w1, w2, offs, hz, n1, n2, out):
    nc = tc.nc
    with ExitStack() as ctx:
        keep = ctx.enter_context(tc.tile_pool(name="keep", bufs=1))
        psum = ctx.enter_context(tc.psum_pool(name="psum", bufs=1))

        def load_list(name, src):
            tile = keep.tile(list(src.shape), U16, name=name)
            nc.sync.dma_start(tile[:], src)
            return tile

        def load_weight(name, w, piece, tag=None, queue=nc.sync):
            c0, width = PIECES[piece]
            raw = keep.tile([P, PACK, width], F32, name=f"{name}_raw{piece}", tag=tag or f"{name}_raw{piece}", align_bytes=64)
            queue.dma_start(out=raw[:], in_=w[:, c0 : c0 + width].rearrange("(p j) c -> p j c", j=PACK))
            return raw

        def interleave(name, raw, b, on_scalar, tag=None):
            c0 = b % 2 * P
            grouped = keep.tile([P, P, PACK], BF16, name=f"{name}_bf{b}", tag=tag or f"{name}_bf{b}", align_bytes=64)
            dst = grouped[:].rearrange("p (c i) j -> p c j i", i=4)
            src = raw[:, :, c0 : c0 + P].rearrange("p j (c i) -> p c j i", i=4)
            if on_scalar:
                nc.scalar.copy(out=dst, in_=src)
            else:
                nc.vector.tensor_copy(out=dst, in_=src)
            return grouped

        def quantise(name, grouped, b):
            codes = keep.tile([P, P], U32, name=f"{name}_codes{b}", tag=f"{name}_codes{b}", align_bytes=64)
            scales = keep.tile([P, P], U8, name=f"{name}_scales{b}", tag=f"{name}_scales{b}", align_bytes=64)
            nc.vector.quantize_mx(out=codes[:].bitcast(FP8X4), scales=scales[:], in_=grouped[:].rearrange("p c j -> p (c j)"))
            return codes, scales

        scale_table = keep.tile([P, T], U8, name="scale_table", tag="scale_table", align_bytes=64)
        nc.vector.memset(scale_table[:].bitcast(I32), 0)
        x_plane = keep.tile([P, 2 * S], U8, name="x_plane", align_bytes=64)
        nc.vector.memset(x_plane[:].bitcast(I32), 0)
        offs_t = load_list("offs_t", offs)
        w1_raw = [load_weight("w1", w1, 0, queue=nc.scalar)]
        hz_t = load_list("hz_t", hz)
        n1_t = load_list("n1_t", n1)
        n2_t = load_list("n2_t", n2)
        scale_rows = x_scales[0].bitcast(I32).rearrange("(r e) c -> e r c", e=2)
        for e in range(2):
            nc.sync.dma_start(out=scale_table[e:P:16, :].bitcast(I32), in_=scale_rows[e])

        word_table = keep.tile([P, T], U32, name="word_table", align_bytes=64)
        nc.sync.dma_start(out=word_table[:].bitcast(I32), in_=x_words[0].rearrange("p c r -> p (c r)").bitcast(I32))
        w2_raw = [load_weight("w2", w2, 0)]

        picked_bytes = keep.tile([P, 2 * S], U8, name="picked_bytes", tag="picked_bytes", align_bytes=64)
        nc.vector.tensor_copy(picked_bytes[:, 0:S], scale_table[:].indirect(offs_t[:]))
        nc.vector.tensor_copy(picked_bytes[:, S : 2 * S], scale_table[:].indirect(hz_t[:]))
        w1_bf0 = interleave("w1", w1_raw[0], 0, True)
        for e in range(2):
            nc.scalar.dma_start(out=x_plane[2 + e : P : 32, :].bitcast(I32), in_=picked_bytes[16 + e : P : 32, :].bitcast(I32))
        for q in range(0, P, 32):
            nc.vector.tensor_copy(x_plane[q : q + 2, :].bitcast(I32), picked_bytes[q : q + 2, :].bitcast(I32))
        late = keep.tile([P, 2 * PACK * (N - 2 * P)], F32, name="late", tag="scale_table", align_bytes=64)
        at = 0
        for c0, width in PIECES[1:]:
            for w, raws in ((w1, w1_raw), (w2, w2_raw)):
                raw = late[:, at : at + PACK * width].rearrange("p (j c) -> p j c", j=PACK)
                nc.scalar.dma_start(out=raw, in_=w[:, c0 : c0 + width].rearrange("(p j) c -> p j c", j=PACK))
                raws.append(raw)
                at += PACK * width

        w1_bf1 = interleave("w1", w1_raw[0], 1, False)
        w1_q = [quantise("w1", w1_bf0, 0), quantise("w1", w1_bf1, 1)]
        words_offs = keep.tile([P, S], U32, name="words_offs", align_bytes=64)
        words_hz = keep.tile([P, S], U32, name="words_hz", align_bytes=64)
        nc.vector.tensor_copy(words_offs[:], word_table[:].indirect(offs_t[:]))
        nc.vector.tensor_copy(words_hz[:], word_table[:].indirect(hz_t[:]))
        w2_bf0 = interleave("w2", w2_raw[0], 0, False)
        w2_bf1 = interleave("w2", w2_raw[0], 1, True)
        w2_q = [quantise("w2", w2_bf0, 0), quantise("w2", w2_bf1, 1)]

        def product(b):
            acc = psum.tile([P, S], F32, name=f"acc{b}")
            nc.tensor.matmul_mx(
                out=acc[:], lhsT=w1_q[b][0][:].bitcast(FP8X4), lhsT_scale=w1_q[b][1][:],
                rhs=words_offs[:].bitcast(FP8X4), rhs_scale=x_plane[:, 0:S], start=True, stop=False)
            nc.tensor.matmul_mx(
                out=acc[:], lhsT=w2_q[b][0][:].bitcast(FP8X4), lhsT_scale=w2_q[b][1][:],
                rhs=words_hz[:].bitcast(FP8X4), rhs_scale=x_plane[:, S : 2 * S], start=False, stop=True)
            h = keep.tile([P, S], F32, name=f"h{b}", tag=f"h{b}", align_bytes=64)
            if b == 0:
                nc.scalar.copy(out=h[:], in_=acc[:])
            else:
                nc.vector.tensor_copy(h[:], acc[:])
            return h

        def fetch(b, h):
            pa = keep.tile([P, W], F32, name=f"pa{b}", align_bytes=64)
            pb = keep.tile([P, W], F32, name=f"pb{b}", align_bytes=64)
            nc.scalar.activation(pa[:], h[:].indirect(n1_t[:]), COPY)
            nc.scalar.activation(pb[:], h[:].indirect(n2_t[:]), COPY)
            return pa, pb

        def combine(name, b, pair, op, tag):
            values = keep.tile([P, W], F32, name=f"{name}{b}", tag=tag, align_bytes=64)
            nc.vector.tensor_tensor(values[:], pair[0][:], pair[1][:], op)
            return values

        def prepare(b):
            w1_bf = interleave("w1", w1_raw[1], b, False)
            w2_bf = interleave("w2", w2_raw[1], b, False)
            w1_q.append(quantise("w1", w1_bf, b))
            w2_q.append(quantise("w2", w2_bf, b))

        def finish(a, h_a, h_b):
            b = a + 1
            pair_a = fetch(a, h_a)
            pair_b = fetch(b, h_b)
            total_a = combine("total", a, pair_a, ADD, f"w2_codes{b}")
            total_b = combine("total", b, pair_b, ADD, f"total{b}")
            diff_a = combine("diff", a, pair_a, SUB, f"h{b}")
            diff_b = combine("diff", b, pair_b, SUB, f"diff{b}")
            result_a = keep.tile([P, S], F32, name=f"result{a}", align_bytes=64)
            result_b = keep.tile([P, S], F32, name=f"result{b}", align_bytes=64)
            nc.scalar.activation(result_a[:].indirect(n1_t[:]), total_a[:], COPY, scale=0.75)
            nc.scalar.activation(result_b[:].indirect(n1_t[:]), total_b[:], COPY, scale=0.75)
            nc.scalar.activation(result_a[:].indirect(n2_t[:]), diff_a[:], COPY)
            nc.sync.dma_start(out=out[a * P : (a + 1) * P, :], in_=result_a[:])
            nc.scalar.activation(result_b[:].indirect(n2_t[:]), diff_b[:], COPY)
            nc.sync.dma_start(out=out[b * P : (b + 1) * P, :], in_=result_b[:])

        h0 = product(0)
        h1 = product(1)
        finish(0, h0, h1)
        prepare(2)
        h2 = product(2)
        prepare(3)
        h3 = product(3)
        finish(2, h2, h3)
